import numpy as np
import ml_dtypes


def mxq(x, axis, fmt="e4m3"):
    dtype, down = {"e4m3": (ml_dtypes.float8_e4m3fn, 7), "e5m2": (ml_dtypes.float8_e5m2, 14)}[fmt]
    v = np.moveaxis(np.asarray(x, np.float32).astype(ml_dtypes.bfloat16).astype(np.float64), axis, -1)
    blocks = v.reshape(v.shape[:-1] + (-1, 32))
    amax = np.abs(blocks).max(-1, keepdims=True)
    byte = np.maximum(np.where(amax > 0, np.frexp(amax)[1] - 1 + 127, 0) - down, 1)
    scale = np.exp2(byte - 127.0)
    codes = (blocks / scale).astype(np.float32).astype(dtype).astype(np.float64)
    return np.moveaxis((codes * scale).reshape(v.shape), -1, axis)


WIDE = False


def mx_kscale(k):
    if not WIDE:
        return np.ones(k)
    levels = np.array([10, -10, 5, -5, 0])
    if k % 512:
        return np.exp2(np.random.permutation(np.resize(levels, k // 32))).repeat(32)
    a = np.empty((k // 512, 16))
    for p in range(k // 512):
        a[p, :8] = np.random.permutation(np.resize(levels, 8))
        for g in range(8):
            far = levels[np.abs(levels - a[p, g]) >= 10]
            a[p, g + 8] = far[np.random.randint(len(far))]
    return np.exp2(a.ravel()).repeat(32)


def f64(x):
    return np.asarray(x).astype(np.float64)


def striped(idx):
    return np.tile(idx.reshape(-1, 16).T, (8, 1)).astype(np.uint16)


def unstriped(offs):
    return offs[:16].T.reshape(-1).astype(np.int64)


E2M1 = np.array([0.0, 0.5, 1.0, 1.5, 2.0, 3.0, 4.0, 6.0, -0.0, -0.5, -1.0, -1.5, -2.0, -3.0, -4.0, -6.0])


def pack_weight(w, fmt):
    k, n = w.shape
    w = f64(np.asarray(w, np.float32).astype(ml_dtypes.bfloat16)).reshape(k // 32, 32, n)
    amax = np.abs(w).max(1)
    if fmt == "e4m3":
        byte = np.frexp(amax)[1] - 1 + 127 - 7
    else:
        mant, ex = np.frexp(amax / 6.0)
        byte = np.where(mant > 0.5, ex, ex - 1) + 127
    byte = np.clip(np.where(amax > 0, byte, 1), 1, 254)
    scaled = (w * np.exp2(127.0 - byte)[:, None, :]).reshape(k, n).astype(np.float32)
    by_word = np.ascontiguousarray(scaled.reshape(k // 512, 128, 4, n).transpose(0, 1, 3, 2))
    if fmt == "e4m3":
        words = by_word.astype(ml_dtypes.float8_e4m3fn).view(np.uint8)
    else:
        c = by_word.astype(ml_dtypes.float4_e2m1fn).view(np.uint8) & 0xF
        words = (c[..., 0::2] | (c[..., 1::2] << 4)).reshape(k // 512, 128, 2 * n)
    return np.ascontiguousarray(words), np.ascontiguousarray(byte.astype(np.uint8).reshape(k // 512, 16, n))


def unpack_weight(words, scales, fmt):
    g, _, n = scales.shape
    words = np.ascontiguousarray(words).reshape(g, 128, n, -1)
    if fmt == "e4m3":
        vals = words.view(ml_dtypes.float8_e4m3fn).astype(np.float64)
    else:
        nib = np.empty((g, 128, n, 4), np.uint8)
        nib[..., 0::2] = words & 0xF
        nib[..., 1::2] = words >> 4
        vals = E2M1[nib]
    vals = vals * np.repeat(np.exp2(scales.astype(np.float64) - 127.0), 8, axis=1)[..., None]
    return vals.transpose(0, 1, 3, 2).reshape(g * 512, n)


def gelu(v):
    return 0.5 * v * (1.0 + np.tanh(np.sqrt(2.0 / np.pi) * (v + 0.044715 * v**3)))


def striped8(idx):
    return np.concatenate([v.reshape(-1, 16).T for v in idx]).astype(np.uint16)


def unstriped8(offs):
    return np.stack([offs[16 * g:16 * g + 16].T.reshape(-1) for g in range(8)]).astype(np.int64)


def runs(v, idx8):
    k = np.arange(v.shape[0])
    return v[k[:, None], idx8[k % 512 // 64]]


K, T, S, H, P, N = 1024, 2048, 1024, 1024, 512, 384

def setup_inputs():
    n = np.random.standard_normal
    s = mx_kscale(K)[:, None]
    u = mx_kscale(H)[:, None]
    d = {}
    d["tab_words"], d["tab_scales"] = pack_weight(n((K, T)) * s, "e4m3")
    d["offs"] = striped8(np.stack([np.random.permutation(T)[:S] for _ in range(8)]))
    d["w1"] = (1.3 * n((K, H)) / s / K ** 0.5).astype(np.float32)
    d["w4_words"], d["w4_scales"] = pack_weight(1.3 * n((K, H)) / s / K ** 0.5, "e2m1")
    d["gain"] = (np.exp(0.3 * n(H)) * u[:, 0]).astype(np.float32)
    d["pos1"] = striped(np.random.permutation(S)[:P])
    d["pos2"] = striped(np.random.permutation(S)[:P])
    d["w3"] = (n((H, N)) / u / H ** 0.5).astype(np.float32)
    d["w5_words"], d["w5_scales"] = pack_weight(0.6 * n((H, N)) / u / H ** 0.5, "e4m3")
    return d

def reference(tab_words, tab_scales, offs, w1, w4_words, w4_scales, gain, pos1, pos2, w3, w5_words, w5_scales):
    v = runs(unpack_weight(tab_words, tab_scales, "e4m3"), unstriped8(offs))
    fresh = mxq(f64(w1), 0, "e4m3").T @ v
    house = unpack_weight(w4_words, w4_scales, "e2m1").T @ v
    h = f64(gain)[:, None] * np.log(1.0 + np.square(fresh - house))
    h1 = h[:, unstriped(pos1)]
    h2 = h[:, unstriped(pos2)]
    worst = mxq(np.maximum(h1, h2), 0, "e4m3")
    both = mxq(h1 + h2, 0, "e4m3")
    top = mxq(f64(w3), 0, "e4m3").T @ worst
    joint = unpack_weight(w5_words, w5_scales, "e4m3").T @ both
    return top - joint

@@ -1,0 +1,244 @@
+from contextlib import ExitStack
+
+import concourse.mybir as mybir
+
+K, T, S, H, PAIRS, N = 1024, 2048, 1024, 1024, 512, 384
+FLOPS = 2 * (2 * K * H * S + 2 * H * N * PAIRS)
+
+F32 = mybir.dt.float32
+BF16 = mybir.dt.bfloat16
+I32 = mybir.dt.int32
+U32 = mybir.dt.uint32
+U16 = mybir.dt.uint16
+U8 = mybir.dt.uint8
+E4M3 = mybir.dt.float8_e4m3fn_x4
+E2M1 = mybir.dt.float4_e2m1fn_x4
+ACT = mybir.ActivationFunctionType
+ALU = mybir.AluOpType
+
+P = 128
+PACK = 4
+KP = P * PACK
+BANK = 512
+
+
+def tile_list_sneaker_doubt_pairs_kernel(tc, tab_words, tab_scales, offs, w1, w4_words, w4_scales, gain,
+                                                  pos1, pos2, w3, w5_words, w5_scales, out):
+    nc = tc.nc
+    with ExitStack() as ctx:
+        keep = ctx.enter_context(tc.tile_pool(name="keep", bufs=1))
+        ring = ctx.enter_context(tc.tile_pool(name="ring", bufs=2))
+        hring = ctx.enter_context(tc.tile_pool(name="hring", bufs=4))
+        psum = ctx.enter_context(tc.psum_pool(name="psum", bufs=8))
+
+        def held(shape, dtype, name, tag=None):
+            return keep.tile(shape, dtype, name=name, tag=tag or name, align_bytes=64)
+
+        offs_sb = keep.tile([P, S // 16], U16, name="offs_sb")
+        pos1_sb = keep.tile([P, PAIRS // 16], U16, name="pos1_sb")
+        pos2_sb = keep.tile([P, PAIRS // 16], U16, name="pos2_sb")
+
+        sc_win = held([P, T], U8, "sc_win", "stage1")
+        w4s_raw = held([P, 2, H], U8, "w4s_raw")
+        v_plane = held([P, 2, S], U8, "v_plane")
+        w5_plane = held([P, 2, N], U8, "w5_plane")
+        nc.vector.memset(sc_win[:].bitcast(I32), 0)
+        nc.vector.memset(w4s_raw[:].rearrange("p a c -> p (a c)").bitcast(I32), 0)
+        one = held([P, 1], F32, "one")
+        zero = held([P, 1], F32, "zero")
+        nc.vector.memset(one[:], 1.0)
+        nc.vector.memset(v_plane[:].rearrange("p a c -> p (a c)").bitcast(I32), 0)
+        nc.vector.memset(w5_plane[:].rearrange("p a c -> p (a c)").bitcast(I32), 0)
+
+        nc.sync.dma_start(sc_win[0:P:4, :].bitcast(I32), tab_scales.rearrange("a q t -> q a t").bitcast(I32))
+        nc.sync.dma_start(offs_sb[:], offs)
+        nc.sync.dma_start(pos1_sb[:], pos1)
+        nc.sync.dma_start(pos2_sb[:], pos2)
+        gain_sb = held([P, 2, PACK], F32, "gain_sb")
+        for d in range(4):
+            nc.scalar.dma_start(w4s_raw[32 * d:32 * d + 4, :, :].bitcast(I32),
+                                w4_scales[:, 4 * d:4 * d + 4, :].rearrange("a r c -> r a c").bitcast(I32))
+        nc.scalar.activation(zero[:], one[:], ACT.Ln)
+        nc.gpsimd.dma_start(gain_sb[:], gain.rearrange("(b p t) -> p b t", b=2, t=PACK))
+        for d in range(4):
+            nc.gpsimd.dma_start(w5_plane[32 * d:32 * d + 4, :, :].bitcast(I32),
+                                w5_scales[:, 4 * d:4 * d + 4, :].rearrange("b r n -> r b n").bitcast(I32))
+
+        tw = [held([P, T], U32, "tw%d" % a) for a in range(2)]
+        for a in range(2):
+            nc.sync.dma_start(tw[a][:].bitcast(I32), tab_words[a].rearrange("p t i -> p (t i)").bitcast(I32))
+
+        def load_w1(a, b, slot):
+            raw = held([P, PACK, KP], F32, "w1raw%d_%d" % (a, b), slot)
+            nc.sync.dma_start(raw[:], w1[a * KP:(a + 1) * KP, b * KP:(b + 1) * KP].rearrange("(p j) c -> p j c", j=PACK))
+            return raw
+
+        def load_w4(b):
+            raw = held([P, 2, KP], U16, "w4raw%d" % b, "stage2")
+            nc.sync.dma_start(raw[:].bitcast(I32),
+                              w4_words[:, :, 2 * b * KP:2 * (b + 1) * KP].rearrange("a p c -> p a c").bitcast(I32))
+            return raw
+
+        w1_bf = {}
+        w1_codes = {}
+        w1_plane = {}
+
+        def cast_w1(a, b, raw, m0, m1, on_vector):
+            if (a, b) not in w1_bf:
+                w1_bf[(a, b)] = held([P, PACK, P, PACK], BF16, "w1bf%d_%d" % (a, b))
+            dst = w1_bf[(a, b)][:, :, m0:m1, :].rearrange("p t m j -> p m j t")
+            src = raw[:, :, PACK * m0:PACK * m1].rearrange("p j (m t) -> p m j t", t=PACK)
+            if on_vector:
+                nc.vector.tensor_scalar(dst, src, -1.0, None, ALU.mult)
+            else:
+                nc.scalar.activation(dst, src, ACT.Copy, scale=-1.0)
+
+        def quant_w1(a, b, cuts):
+            w1_codes[(a, b)] = held([P, KP], U32, "w1c%d_%d" % (a, b))
+            w1_plane[(a, b)] = held([P, KP], U8, "w1s%d_%d" % (a, b))
+            flat = w1_bf[(a, b)][:].rearrange("p t m j -> p (t m j)")
+            for c0, c1 in zip(cuts[:-1], cuts[1:]):
+                nc.vector.quantize_mx(w1_codes[(a, b)][:, c0:c1].bitcast(E4M3), w1_plane[(a, b)][:, c0:c1],
+                                      flat[:, PACK * c0:PACK * c1])
+
+        w4_codes = [held([P, 2, KP], U16, "w4c%d" % b) for b in range(2)]
+        w4_plane = [held([P, 2, KP], U8, "w4p%d" % b) for b in range(2)]
+
+        def deal_w4(b, raw):
+            nc.vector.tensor_copy(w4_codes[b][:].rearrange("p a (t m) -> p a t m", t=PACK),
+                                  raw[:].rearrange("p a (m t) -> p a t m", t=PACK))
+            nc.vector.tensor_copy(w4_plane[b][:].rearrange("p a (t m) -> p a t m", t=PACK),
+                                  w4s_raw[:, :, b * KP:(b + 1) * KP].rearrange("p a (m t) -> p a t m", t=PACK))
+
+        raw00 = load_w1(0, 0, "stage0")
+        w4raw0 = load_w4(0)
+
+        sc_got = held([P, S], U8, "sc_got", "stage3")
+        nc.vector.tensor_copy(sc_got[:], sc_win[:].indirect(offs_sb[:]))
+        for d in range(4):
+            nc.scalar.dma_start(v_plane[32 * d:32 * d + 4, :, :].bitcast(I32),
+                                sc_got[32 * d:32 * d + 32:4, :].bitcast(I32))
+        raw10 = load_w1(1, 0, "stage1")
+        raw01 = load_w1(0, 1, "stage3")
+        v_codes = [held([P, S], U32, "v_codes%d" % a) for a in range(2)]
+        for a in range(2):
+            nc.vector.tensor_copy(v_codes[a][:], tw[a][:].indirect(offs_sb[:]))
+
+        deal_w4(0, w4raw0)
+        cast_w1(0, 0, raw00, 0, P, False)
+        quant_w1(0, 0, (0, KP))
+        w4raw1 = load_w4(1)
+        raw11 = load_w1(1, 1, "stage0")
+        cast_w1(1, 0, raw10, 0, P // 2, False)
+        cast_w1(1, 0, raw10, P // 2, P, True)
+        quant_w1(1, 0, (0, P, 2 * P, KP))
+        deal_w4(1, w4raw1)
+
+        w5_codes = held([P, 2, N], U32, "w5_codes", "stage2")
+        nc.sync.dma_start(w5_codes[:].bitcast(I32), w5_words.rearrange("b p n i -> p b (n i)").bitcast(I32))
+
+        def load_w3(b):
+            raw = held([P, PACK, N], F32, "w3raw%d" % b, ("stage1", "stage3")[b])
+            nc.sync.dma_start(raw[:], w3[b * KP:(b + 1) * KP, :].rearrange("(p j) n -> p j n", j=PACK))
+            return raw
+
+        w3raw = [load_w3(0)]
+
+        def stage1(b, t, h1, h2):
+            cols = slice(t * P, (t + 1) * P)
+            if b == 0 and t >= 2:
+                sq = held([P, S], F32, "sq0%d" % t, ("stage3", "stage0")[t - 2])
+            else:
+                sq = ring.tile([P, S], F32, name="sq")
+            for half in range(S // BANK):
+                js = slice(half * BANK, (half + 1) * BANK)
+                acc = psum.tile([P, BANK], F32, name="acc")
+                passes = [
+                    (w4_codes[b][:, 0, cols].bitcast(E2M1), w4_plane[b][:, 0, cols], 0),
+                    (w4_codes[b][:, 1, cols].bitcast(E2M1), w4_plane[b][:, 1, cols], 1),
+                    (w1_codes[(0, b)][:, cols].bitcast(E4M3), w1_plane[(0, b)][:, cols], 0),
+                    (w1_codes[(1, b)][:, cols].bitcast(E4M3), w1_plane[(1, b)][:, cols], 1),
+                ]
+                for i, (codes, plane, a) in enumerate(passes):
+                    nc.tensor.matmul_mx(acc[:], lhsT=codes, lhsT_scale=plane, rhs=v_codes[a][:, js].bitcast(E4M3),
+                                        rhs_scale=v_plane[:, a, js], start=(i == 0), stop=(i == len(passes) - 1))
+                nc.scalar.activation(sq[:, js], acc[:], ACT.Square, bias=zero[:])
+            lg = hring.tile([P, S], F32, name="lg")
+            nc.scalar.activation(lg[:], sq[:], ACT.Ln, bias=1.0)
+            h = hring.tile([P, S], F32, name="h")
+            if b == 0 and t < 3:
+                nc.vector.tensor_scalar(h[:], lg[:], gain_sb[:, b, t:t + 1], None, ALU.mult)
+            else:
+                nc.scalar.activation(h[:], lg[:], ACT.Copy, scale=gain_sb[:, b, t:t + 1])
+            nc.vector.tensor_copy(h1[:, t, :], h[:].indirect(pos1_sb[:]))
+            nc.vector.tensor_copy(h2[:, t, :], h[:].indirect(pos2_sb[:]))
+
+        HALF = PAIRS // 2
+
+        def join(b, half, h1, h2):
+            ms = slice(half * HALF, (half + 1) * HALF)
+            bf = ring.tile([P, 2, HALF, PACK], BF16, name="pair_bf", align_bytes=64)
+            for i, op in enumerate((ALU.max, ALU.add)):
+                nc.vector.tensor_tensor(bf[:, i, :, :].rearrange("p (c i) t -> p c t i", i=4),
+                                        h1[:, :, ms].rearrange("p t (c i) -> p c t i", i=4),
+                                        h2[:, :, ms].rearrange("p t (c i) -> p c t i", i=4), op)
+            return bf
+
+        def quant_pair(b, half, bf):
+            codes = held([P, 2 * HALF], U32, "pair_codes%d_%d" % (b, half))
+            plane = held([P, 2 * HALF], U8, "pair_plane%d_%d" % (b, half))
+            nc.vector.quantize_mx(codes[:].bitcast(E4M3), plane[:], bf[:].rearrange("p i m t -> p (i m t)"))
+            return codes, plane
+
+        pairs = {}
+        picked = []
+        for b in range(2):
+            h1 = ring.tile([P, PACK, PAIRS], F32, name="h1")
+            h2 = ring.tile([P, PACK, PAIRS], F32, name="h2")
+            picked.append((h1, h2))
+            for t in range(PACK):
+                stage1(b, t, h1, h2)
+                if b == 0 and t in (1, 2):
+                    cast_w1(t - 1, 1, (raw01, raw11)[t - 1], 0, P, False)
+                    quant_w1(t - 1, 1, (0, KP))
+                if b == 0 and t == 2:
+                    w3raw.append(load_w3(1))
+            if b == 0:
+                made = [join(0, half, h1, h2) for half in range(2)]
+                for half in range(2):
+                    pairs[(0, half)] = quant_pair(0, half, made[half])
+
+        w3_bf = held([P, 2, N, PACK], BF16, "w3_bf")
+        w3_codes = held([P, 2 * N], U32, "w3_codes")
+        w3_plane = held([P, 2 * N], U8, "w3_plane")
+        for b in range(2):
+            nc.scalar.activation(
+                w3_bf[:, b, :, :].rearrange("p (c i) j -> p c j i", i=4),
+                w3raw[b][:].rearrange("p j (c i) -> p c j i", i=4), ACT.Copy, scale=-1.0)
+        first = join(1, 0, h1, h2)
+        flat = w3_bf[:].rearrange("p b n j -> p (b n j)")
+        for c0, width in ((0, 512), (512, 256)):
+            nc.vector.quantize_mx(w3_codes[:, c0:c0 + width].bitcast(E4M3), w3_plane[:, c0:c0 + width],
+                                  flat[:, PACK * c0:PACK * (c0 + width)])
+        pairs[(1, 0)] = quant_pair(1, 0, first)
+        pairs[(1, 1)] = quant_pair(1, 1, join(1, 1, h1, h2))
+
+        for half in range(2):
+            for n in range(N // P):
+                acc = psum.tile([P, HALF], F32, name="acc")
+                for b in range(2):
+                    codes, plane = pairs[(b, half)]
+                    cols3 = slice(b * N + n * P, b * N + (n + 1) * P)
+                    cols5 = slice(n * P, (n + 1) * P)
+                    weights = [(w3_codes[:, cols3], w3_plane[:, cols3]), (w5_codes[:, b, cols5], w5_plane[:, b, cols5])]
+                    for i, (w_codes, w_plane) in enumerate(weights):
+                        ms = slice(i * HALF, (i + 1) * HALF)
+                        nc.tensor.matmul_mx(acc[:], lhsT=w_codes.bitcast(E4M3), lhsT_scale=w_plane,
+                                            rhs=codes[:, ms].bitcast(E4M3), rhs_scale=plane[:, ms],
+                                            start=(b == 0 and i == 0), stop=(b == 1 and i == 1))
+                res = held([P, HALF], F32, "res%d_%d" % (half, n))
+                if half == 1 and n == 1:
+                    nc.vector.tensor_scalar(res[:], acc[:], -1.0, None, ALU.mult)
+                else:
+                    nc.scalar.activation(res[:], acc[:], ACT.Copy, scale=-1.0)
+                nc.sync.dma_start(out[n * P:(n + 1) * P, half * HALF:(half + 1) * HALF], res[:])

@@ -56,7 +56,7 @@ def tile_list_sneaker_doubt_pairs_kernel(tc, tab_words, tab_scales, offs, w1, w4
         nc.sync.dma_start(pos2_sb[:], pos2)
         gain_sb = held([P, 2, PACK], F32, "gain_sb")
         for d in range(4):
-            nc.scalar.dma_start(w4s_raw[32 * d:32 * d + 4, :, :].bitcast(I32),
+            nc.sync.dma_start(w4s_raw[32 * d:32 * d + 4, :, :].bitcast(I32),
                                 w4_scales[:, 4 * d:4 * d + 4, :].rearrange("a r c -> r a c").bitcast(I32))
         nc.scalar.activation(zero[:], one[:], ACT.Ln)
         nc.gpsimd.dma_start(gain_sb[:], gain.rearrange("(b p t) -> p b t", b=2, t=PACK))
@@ -65,7 +65,8 @@ def tile_list_sneaker_doubt_pairs_kernel(tc, tab_words, tab_scales, offs, w1, w4
                                 w5_scales[:, 4 * d:4 * d + 4, :].rearrange("b r n -> r b n").bitcast(I32))
 
         tw = [held([P, T], U32, "tw%d" % a) for a in range(2)]
-        for a in range(2):
+
+        def load_tab(a):
             nc.sync.dma_start(tw[a][:].bitcast(I32), tab_words[a].rearrange("p t i -> p (t i)").bitcast(I32))
 
         def load_w1(a, b, slot):
@@ -73,8 +74,8 @@ def tile_list_sneaker_doubt_pairs_kernel(tc, tab_words, tab_scales, offs, w1, w4
             nc.sync.dma_start(raw[:], w1[a * KP:(a + 1) * KP, b * KP:(b + 1) * KP].rearrange("(p j) c -> p j c", j=PACK))
             return raw
 
-        def load_w4(b):
-            raw = held([P, 2, KP], U16, "w4raw%d" % b, "stage2")
+        def load_w4(b, slot):
+            raw = held([P, 2, KP], U16, "w4raw%d" % b, slot)
             nc.sync.dma_start(raw[:].bitcast(I32),
                               w4_words[:, :, 2 * b * KP:2 * (b + 1) * KP].rearrange("a p c -> p a c").bitcast(I32))
             return raw
@@ -87,7 +88,7 @@ def tile_list_sneaker_doubt_pairs_kernel(tc, tab_words, tab_scales, offs, w1, w4
             if (a, b) not in w1_bf:
                 w1_bf[(a, b)] = held([P, PACK, P, PACK], BF16, "w1bf%d_%d" % (a, b))
             dst = w1_bf[(a, b)][:, :, m0:m1, :].rearrange("p t m j -> p m j t")
-            src = raw[:, :, PACK * m0:PACK * m1].rearrange("p j (m t) -> p m j t", t=PACK)
+            src = raw.rearrange("p j (m t) -> p m j t", t=PACK)
             if on_vector:
                 nc.vector.tensor_scalar(dst, src, -1.0, None, ALU.mult)
             else:
@@ -102,54 +103,65 @@ def tile_list_sneaker_doubt_pairs_kernel(tc, tab_words, tab_scales, offs, w1, w4
                                       flat[:, PACK * c0:PACK * c1])
 
         w4_codes = [held([P, 2, KP], U16, "w4c%d" % b) for b in range(2)]
-        w4_plane = [held([P, 2, KP], U8, "w4p%d" % b) for b in range(2)]
 
-        def deal_w4(b, raw):
-            nc.vector.tensor_copy(w4_codes[b][:].rearrange("p a (t m) -> p a t m", t=PACK),
-                                  raw[:].rearrange("p a (m t) -> p a t m", t=PACK))
+        def deal_w4_words(b, raw, t0, t1):
+            nc.vector.tensor_copy(w4_codes[b][:].rearrange("p a (t m) -> p a t m", t=PACK)[:, :, t0:t1, :],
+                                  raw[:].rearrange("p a (m t) -> p a t m", t=PACK)[:, :, t0:t1, :])
+
+        def place_rows(plane, rows):
+            for d in range(4):
+                nc.sync.dma_start(plane[32 * d:32 * d + 4, :, :].bitcast(I32),
+                                    rows[32 * d:32 * d + 32:4, :].bitcast(I32))
+
+        load_tab(0)
+        load_tab(1)
+        w4raw0 = load_w4(0, "stage2")
+        raw00 = load_w1(0, 0, "stage0")
+
+        sc_got = held([P, S], U8, "sc_got")
+        nc.vector.tensor_copy(sc_got[:], sc_win[:].indirect(offs_sb[:]))
+        place_rows(v_plane, sc_got)
+        raw10 = held([P, 2, PACK, KP // 2], F32, "w1raw1_0", "stage1")
+        for u in range(2):
+            nc.sync.dma_start(raw10[:, u, :, :],
+                              w1[KP:2 * KP, u * (KP // 2):(u + 1) * (KP // 2)].rearrange("(p j) c -> p j c", j=PACK))
+        w4_plane = {}
+
+        def deal_w4_scales(b, slot):
+            w4_plane[b] = held([P, 2, KP], U8, "w4p%d" % b, slot)
             nc.vector.tensor_copy(w4_plane[b][:].rearrange("p a (t m) -> p a t m", t=PACK),
                                   w4s_raw[:, :, b * KP:(b + 1) * KP].rearrange("p a (m t) -> p a t m", t=PACK))
 
-        raw00 = load_w1(0, 0, "stage0")
-        w4raw0 = load_w4(0)
-
-        sc_got = held([P, S], U8, "sc_got", "stage3")
-        nc.vector.tensor_copy(sc_got[:], sc_win[:].indirect(offs_sb[:]))
-        for d in range(4):
-            nc.scalar.dma_start(v_plane[32 * d:32 * d + 4, :, :].bitcast(I32),
-                                sc_got[32 * d:32 * d + 32:4, :].bitcast(I32))
-        raw10 = load_w1(1, 0, "stage1")
-        raw01 = load_w1(0, 1, "stage3")
         v_codes = [held([P, S], U32, "v_codes%d" % a) for a in range(2)]
         for a in range(2):
             nc.vector.tensor_copy(v_codes[a][:], tw[a][:].indirect(offs_sb[:]))
-
-        deal_w4(0, w4raw0)
-        cast_w1(0, 0, raw00, 0, P, False)
+        deal_w4_scales(0, "w4p0")
+        deal_w4_words(0, w4raw0, 0, PACK)
+        w4raw1 = load_w4(1, "tw0")
+        raw01 = load_w1(0, 1, "tw1")
+        cast_w1(0, 0, raw00[:], 0, P, False)
+        cast_w1(1, 0, raw10[:, 0, :, :], 0, P // 2, True)
         quant_w1(0, 0, (0, KP))
-        w4raw1 = load_w4(1)
+        cast_w1(1, 0, raw10[:, 1, :, :], P // 2, P, False)
         raw11 = load_w1(1, 1, "stage0")
-        cast_w1(1, 0, raw10, 0, P // 2, False)
-        cast_w1(1, 0, raw10, P // 2, P, True)
         quant_w1(1, 0, (0, P, 2 * P, KP))
-        deal_w4(1, w4raw1)
+        deal_w4_scales(1, "w1bf1_0")
+        deal_w4_words(1, w4raw1, 0, PACK)
+        cast_w1(0, 1, raw01[:], 0, P, True)
+        quant_w1(0, 1, (0, KP))
 
-        w5_codes = held([P, 2, N], U32, "w5_codes", "stage2")
-        nc.sync.dma_start(w5_codes[:].bitcast(I32), w5_words.rearrange("b p n i -> p b (n i)").bitcast(I32))
-
-        def load_w3(b):
-            raw = held([P, PACK, N], F32, "w3raw%d" % b, ("stage1", "stage3")[b])
+        def load_w3(b, slot):
+            raw = held([P, PACK, N], F32, "w3raw%d" % b, slot)
             nc.sync.dma_start(raw[:], w3[b * KP:(b + 1) * KP, :].rearrange("(p j) n -> p j n", j=PACK))
             return raw
 
-        w3raw = [load_w3(0)]
+        w3raw = [load_w3(0, "stage1"), load_w3(1, "tw1")]
+        w5_codes = held([P, 2, N], U32, "w5_codes", "stage2")
+        nc.sync.dma_start(w5_codes[:].bitcast(I32), w5_words.rearrange("b p n i -> p b (n i)").bitcast(I32))
 
         def stage1(b, t, h1, h2):
             cols = slice(t * P, (t + 1) * P)
-            if b == 0 and t >= 2:
-                sq = held([P, S], F32, "sq0%d" % t, ("stage3", "stage0")[t - 2])
-            else:
-                sq = ring.tile([P, S], F32, name="sq")
+            sq = ring.tile([P, S], F32, name="sq")
             for half in range(S // BANK):
                 js = slice(half * BANK, (half + 1) * BANK)
                 acc = psum.tile([P, BANK], F32, name="acc")
@@ -163,13 +175,19 @@ def tile_list_sneaker_doubt_pairs_kernel(tc, tab_words, tab_scales, offs, w1, w4
                     nc.tensor.matmul_mx(acc[:], lhsT=codes, lhsT_scale=plane, rhs=v_codes[a][:, js].bitcast(E4M3),
                                         rhs_scale=v_plane[:, a, js], start=(i == 0), stop=(i == len(passes) - 1))
                 nc.scalar.activation(sq[:, js], acc[:], ACT.Square, bias=zero[:])
-            lg = hring.tile([P, S], F32, name="lg")
-            nc.scalar.activation(lg[:], sq[:], ACT.Ln, bias=1.0)
-            h = hring.tile([P, S], F32, name="h")
-            if b == 0 and t < 3:
-                nc.vector.tensor_scalar(h[:], lg[:], gain_sb[:, b, t:t + 1], None, ALU.mult)
+            if (b, t) == (1, 3):
+                lg = held([P, S], F32, "lg13", "late")
             else:
-                nc.scalar.activation(h[:], lg[:], ACT.Copy, scale=gain_sb[:, b, t:t + 1])
+                lg = hring.tile([P, S], F32, name="lg")
+            h = hring.tile([P, S], F32, name="h")
+            step = BANK if (b, t) == (0, 0) else S
+            for j0 in range(0, S, step):
+                js = slice(j0, j0 + step)
+                nc.scalar.activation(lg[:, js], sq[:, js], ACT.Ln, bias=1.0)
+                if b == 0 and t < 2:
+                    nc.vector.tensor_scalar(h[:, js], lg[:, js], gain_sb[:, b, t:t + 1], None, ALU.mult)
+                else:
+                    nc.scalar.activation(h[:, js], lg[:, js], ACT.Copy, scale=gain_sb[:, b, t:t + 1])
             nc.vector.tensor_copy(h1[:, t, :], h[:].indirect(pos1_sb[:]))
             nc.vector.tensor_copy(h2[:, t, :], h[:].indirect(pos2_sb[:]))
 
@@ -198,17 +216,15 @@ def tile_list_sneaker_doubt_pairs_kernel(tc, tab_words, tab_scales, offs, w1, w4
             picked.append((h1, h2))
             for t in range(PACK):
                 stage1(b, t, h1, h2)
-                if b == 0 and t in (1, 2):
-                    cast_w1(t - 1, 1, (raw01, raw11)[t - 1], 0, P, False)
-                    quant_w1(t - 1, 1, (0, KP))
-                if b == 0 and t == 2:
-                    w3raw.append(load_w3(1))
+                if b == 0 and t == 1:
+                    cast_w1(1, 1, raw11[:], 0, P, True)
+                    quant_w1(1, 1, (0, KP))
             if b == 0:
                 made = [join(0, half, h1, h2) for half in range(2)]
                 for half in range(2):
                     pairs[(0, half)] = quant_pair(0, half, made[half])
 
-        w3_bf = held([P, 2, N, PACK], BF16, "w3_bf")
+        w3_bf = held([P, 2, N, PACK], BF16, "w3_bf", "late")
         w3_codes = held([P, 2 * N], U32, "w3_codes")
         w3_plane = held([P, 2 * N], U8, "w3_plane")
         for b in range(2):
@@ -226,16 +242,16 @@ def tile_list_sneaker_doubt_pairs_kernel(tc, tab_words, tab_scales, offs, w1, w4
         for half in range(2):
             for n in range(N // P):
                 acc = psum.tile([P, HALF], F32, name="acc")
-                for b in range(2):
+                for b, i in ((0, 1), (0, 0), (1, 0), (1, 1)):
                     codes, plane = pairs[(b, half)]
                     cols3 = slice(b * N + n * P, b * N + (n + 1) * P)
                     cols5 = slice(n * P, (n + 1) * P)
                     weights = [(w3_codes[:, cols3], w3_plane[:, cols3]), (w5_codes[:, b, cols5], w5_plane[:, b, cols5])]
-                    for i, (w_codes, w_plane) in enumerate(weights):
-                        ms = slice(i * HALF, (i + 1) * HALF)
-                        nc.tensor.matmul_mx(acc[:], lhsT=w_codes.bitcast(E4M3), lhsT_scale=w_plane,
-                                            rhs=codes[:, ms].bitcast(E4M3), rhs_scale=plane[:, ms],
-                                            start=(b == 0 and i == 0), stop=(b == 1 and i == 1))
+                    w_codes, w_plane = weights[i]
+                    ms = slice(i * HALF, (i + 1) * HALF)
+                    nc.tensor.matmul_mx(acc[:], lhsT=w_codes.bitcast(E4M3), lhsT_scale=w_plane,
+                                        rhs=codes[:, ms].bitcast(E4M3), rhs_scale=plane[:, ms],
+                                        start=(b == 0 and i == 1), stop=(b == 1 and i == 1))
                 res = held([P, HALF], F32, "res%d_%d" % (half, n))
                 if half == 1 and n == 1:
                     nc.vector.tensor_scalar(res[:], acc[:], -1.0, None, ALU.mult)

@@ -18,8 +18,12 @@ ALU = mybir.AluOpType
 
 P = 128
 PACK = 4
-KP = P * PACK
+PASS = P * PACK
 BANK = 512
+QUADS, QUAD = 4, 32
+LINE = 4
+HALF = PAIRS // 2
+GAINS_ON_VECTOR = 2
 
 
 def tile_list_sneaker_doubt_pairs_kernel(tc, tab_words, tab_scales, offs, w1, w4_words, w4_scales, gain,
@@ -28,233 +32,224 @@ def tile_list_sneaker_doubt_pairs_kernel(tc, tab_words, tab_scales, offs, w1, w4
     with ExitStack() as ctx:
         keep = ctx.enter_context(tc.tile_pool(name="keep", bufs=1))
         ring = ctx.enter_context(tc.tile_pool(name="ring", bufs=2))
-        hring = ctx.enter_context(tc.tile_pool(name="hring", bufs=4))
+        ahead = ctx.enter_context(tc.tile_pool(name="ahead", bufs=PACK))
         psum = ctx.enter_context(tc.psum_pool(name="psum", bufs=8))
 
-        def held(shape, dtype, name, tag=None):
-            return keep.tile(shape, dtype, name=name, tag=tag or name, align_bytes=64)
+        def held(shape, dtype, name, slot=None):
+            return keep.tile(shape, dtype, name=name, tag=slot or name, align_bytes=64)
 
         offs_sb = keep.tile([P, S // 16], U16, name="offs_sb")
         pos1_sb = keep.tile([P, PAIRS // 16], U16, name="pos1_sb")
         pos2_sb = keep.tile([P, PAIRS // 16], U16, name="pos2_sb")
 
-        sc_win = held([P, T], U8, "sc_win", "stage1")
-        w4s_raw = held([P, 2, H], U8, "w4s_raw")
+        tab_rows = held([P, T], U8, "tab_rows", "slot_a")
+        w4_rows = held([P, 2, H], U8, "w4_rows")
         v_plane = held([P, 2, S], U8, "v_plane")
         w5_plane = held([P, 2, N], U8, "w5_plane")
-        nc.vector.memset(sc_win[:].bitcast(I32), 0)
-        nc.vector.memset(w4s_raw[:].rearrange("p a c -> p (a c)").bitcast(I32), 0)
+        nc.vector.memset(tab_rows[:].bitcast(I32), 0)
+        nc.vector.memset(w4_rows[:].rearrange("p a c -> p (a c)").bitcast(I32), 0)
         one = held([P, 1], F32, "one")
         zero = held([P, 1], F32, "zero")
         nc.vector.memset(one[:], 1.0)
         nc.vector.memset(v_plane[:].rearrange("p a c -> p (a c)").bitcast(I32), 0)
         nc.vector.memset(w5_plane[:].rearrange("p a c -> p (a c)").bitcast(I32), 0)
 
-        nc.sync.dma_start(sc_win[0:P:4, :].bitcast(I32), tab_scales.rearrange("a q t -> q a t").bitcast(I32))
+        nc.sync.dma_start(tab_rows[0:P:4, :].bitcast(I32), tab_scales.rearrange("a q t -> q a t").bitcast(I32))
         nc.sync.dma_start(offs_sb[:], offs)
         nc.sync.dma_start(pos1_sb[:], pos1)
         nc.sync.dma_start(pos2_sb[:], pos2)
         gain_sb = held([P, 2, PACK], F32, "gain_sb")
-        for d in range(4):
-            nc.sync.dma_start(w4s_raw[32 * d:32 * d + 4, :, :].bitcast(I32),
-                                w4_scales[:, 4 * d:4 * d + 4, :].rearrange("a r c -> r a c").bitcast(I32))
+
+        def load_scale_rows(queue, plane, scales):
+            for d in range(QUADS):
+                queue.dma_start(plane[QUAD * d:QUAD * d + 4, :, :].bitcast(I32),
+                                scales[:, 4 * d:4 * d + 4, :].rearrange("a q c -> q a c").bitcast(I32))
+
+        load_scale_rows(nc.sync, w4_rows, w4_scales)
         nc.scalar.activation(zero[:], one[:], ACT.Ln)
         nc.gpsimd.dma_start(gain_sb[:], gain.rearrange("(b p t) -> p b t", b=2, t=PACK))
-        for d in range(4):
-            nc.gpsimd.dma_start(w5_plane[32 * d:32 * d + 4, :, :].bitcast(I32),
-                                w5_scales[:, 4 * d:4 * d + 4, :].rearrange("b r n -> r b n").bitcast(I32))
+        load_scale_rows(nc.gpsimd, w5_plane, w5_scales)
 
-        tw = [held([P, T], U32, "tw%d" % a) for a in range(2)]
-
-        def load_tab(a):
-            nc.sync.dma_start(tw[a][:].bitcast(I32), tab_words[a].rearrange("p t i -> p (t i)").bitcast(I32))
+        def load_rows(name, slot, rows):
+            raw = held([P, PACK, rows.shape[1]], F32, name, slot)
+            nc.sync.dma_start(raw[:], rows.rearrange("(p i) c -> p i c", i=PACK))
+            return raw
 
         def load_w1(a, b, slot):
-            raw = held([P, PACK, KP], F32, "w1raw%d_%d" % (a, b), slot)
-            nc.sync.dma_start(raw[:], w1[a * KP:(a + 1) * KP, b * KP:(b + 1) * KP].rearrange("(p j) c -> p j c", j=PACK))
-            return raw
+            return load_rows("w1_raw%d%d" % (a, b), slot, w1[a * PASS:(a + 1) * PASS, b * PASS:(b + 1) * PASS])
 
         def load_w4(b, slot):
-            raw = held([P, 2, KP], U16, "w4raw%d" % b, slot)
+            raw = held([P, 2, PASS], U16, "w4_raw%d" % b, slot)
             nc.sync.dma_start(raw[:].bitcast(I32),
-                              w4_words[:, :, 2 * b * KP:2 * (b + 1) * KP].rearrange("a p c -> p a c").bitcast(I32))
+                              w4_words[:, :, 2 * b * PASS:2 * (b + 1) * PASS].rearrange("a p c -> p a c").bitcast(I32))
             return raw
 
-        w1_bf = {}
-        w1_codes = {}
-        w1_plane = {}
+        w1_bf, w1_codes, w1_plane, w4_plane = {}, {}, {}, {}
 
-        def cast_w1(a, b, raw, m0, m1, on_vector):
-            if (a, b) not in w1_bf:
-                w1_bf[(a, b)] = held([P, PACK, P, PACK], BF16, "w1bf%d_%d" % (a, b))
-            dst = w1_bf[(a, b)][:, :, m0:m1, :].rearrange("p t m j -> p m j t")
-            src = raw.rearrange("p j (m t) -> p m j t", t=PACK)
-            if on_vector:
+        def negate(engine, dst, src):
+            if engine == "vector":
                 nc.vector.tensor_scalar(dst, src, -1.0, None, ALU.mult)
             else:
                 nc.scalar.activation(dst, src, ACT.Copy, scale=-1.0)
 
-        def quant_w1(a, b, cuts):
-            w1_codes[(a, b)] = held([P, KP], U32, "w1c%d_%d" % (a, b))
-            w1_plane[(a, b)] = held([P, KP], U8, "w1s%d_%d" % (a, b))
-            flat = w1_bf[(a, b)][:].rearrange("p t m j -> p (t m j)")
-            for c0, c1 in zip(cuts[:-1], cuts[1:]):
+        def cast_w1(engine, a, b, raw, m0, m1, t0, t1):
+            if (a, b) not in w1_bf:
+                w1_bf[(a, b)] = held([P, PACK, P, PACK], BF16, "w1_bf%d%d" % (a, b))
+            negate(engine, w1_bf[(a, b)][:, t0:t1, m0:m1, :].rearrange("p t m i -> p m i t"),
+                   raw.rearrange("p i (m t) -> p m i t", t=PACK)[:, :, :, t0:t1])
+
+        def quantise_w1(a, b, slices_a_call):
+            w1_codes[(a, b)] = held([P, PASS], U32, "w1_codes%d%d" % (a, b))
+            w1_plane[(a, b)] = held([P, PASS], U8, "w1_plane%d%d" % (a, b))
+            flat = w1_bf[(a, b)][:].rearrange("p t m i -> p (t m i)")
+            for c0 in range(0, PASS, slices_a_call * P):
+                c1 = c0 + slices_a_call * P
                 nc.vector.quantize_mx(w1_codes[(a, b)][:, c0:c1].bitcast(E4M3), w1_plane[(a, b)][:, c0:c1],
                                       flat[:, PACK * c0:PACK * c1])
 
-        w4_codes = [held([P, 2, KP], U16, "w4c%d" % b) for b in range(2)]
+        def deal(dst, src):
+            nc.vector.tensor_copy(dst.rearrange("p a (t m) -> p a t m", t=PACK),
+                                  src.rearrange("p a (m t) -> p a t m", t=PACK))
 
-        def deal_w4_words(b, raw, t0, t1):
-            nc.vector.tensor_copy(w4_codes[b][:].rearrange("p a (t m) -> p a t m", t=PACK)[:, :, t0:t1, :],
-                                  raw[:].rearrange("p a (m t) -> p a t m", t=PACK)[:, :, t0:t1, :])
+        def deal_w4(b, raw, slot):
+            w4_plane[b] = held([P, 2, PASS], U8, "w4_plane%d" % b, slot)
+            deal(w4_plane[b][:], w4_rows[:, :, b * PASS:(b + 1) * PASS])
+            deal(w4_codes[b][:], raw[:])
 
-        def place_rows(plane, rows):
-            for d in range(4):
-                nc.sync.dma_start(plane[32 * d:32 * d + 4, :, :].bitcast(I32),
-                                    rows[32 * d:32 * d + 32:4, :].bitcast(I32))
+        tab = [held([P, T], U32, "tab%d" % a) for a in range(2)]
+        w4_codes = [held([P, 2, PASS], U16, "w4_codes%d" % b) for b in range(2)]
+        for a in range(2):
+            nc.sync.dma_start(tab[a][:].bitcast(I32), tab_words[a].rearrange("p t i -> p (t i)").bitcast(I32))
+        w4_raw0 = load_w4(0, "slot_c")
+        w1_raw00 = load_w1(0, 0, "slot_b")
 
-        load_tab(0)
-        load_tab(1)
-        w4raw0 = load_w4(0, "stage2")
-        raw00 = load_w1(0, 0, "stage0")
-
-        sc_got = held([P, S], U8, "sc_got")
-        nc.vector.tensor_copy(sc_got[:], sc_win[:].indirect(offs_sb[:]))
-        place_rows(v_plane, sc_got)
-        raw10 = held([P, 2, PACK, KP // 2], F32, "w1raw1_0", "stage1")
+        v_rows = held([P, S], U8, "v_rows")
+        nc.vector.tensor_copy(v_rows[:], tab_rows[:].indirect(offs_sb[:]))
+        for d in range(QUADS):
+            nc.sync.dma_start(v_plane[QUAD * d:QUAD * d + 4, :, :].bitcast(I32),
+                              v_rows[QUAD * d:QUAD * (d + 1):4, :].bitcast(I32))
+        w1_raw10 = held([P, 2, PACK, PASS // 2], F32, "w1_raw10", "slot_a")
         for u in range(2):
-            nc.sync.dma_start(raw10[:, u, :, :],
-                              w1[KP:2 * KP, u * (KP // 2):(u + 1) * (KP // 2)].rearrange("(p j) c -> p j c", j=PACK))
-        w4_plane = {}
-
-        def deal_w4_scales(b, slot):
-            w4_plane[b] = held([P, 2, KP], U8, "w4p%d" % b, slot)
-            nc.vector.tensor_copy(w4_plane[b][:].rearrange("p a (t m) -> p a t m", t=PACK),
-                                  w4s_raw[:, :, b * KP:(b + 1) * KP].rearrange("p a (m t) -> p a t m", t=PACK))
-
+            nc.sync.dma_start(w1_raw10[:, u, :, :],
+                              w1[PASS:2 * PASS, u * (PASS // 2):(u + 1) * (PASS // 2)].rearrange("(p i) c -> p i c", i=PACK))
         v_codes = [held([P, S], U32, "v_codes%d" % a) for a in range(2)]
         for a in range(2):
-            nc.vector.tensor_copy(v_codes[a][:], tw[a][:].indirect(offs_sb[:]))
-        deal_w4_scales(0, "w4p0")
-        deal_w4_words(0, w4raw0, 0, PACK)
-        w4raw1 = load_w4(1, "tw0")
-        raw01 = load_w1(0, 1, "tw1")
-        cast_w1(0, 0, raw00[:], 0, P, False)
-        cast_w1(1, 0, raw10[:, 0, :, :], 0, P // 2, True)
-        quant_w1(0, 0, (0, KP))
-        cast_w1(1, 0, raw10[:, 1, :, :], P // 2, P, False)
-        raw11 = load_w1(1, 1, "stage0")
-        quant_w1(1, 0, (0, P, 2 * P, KP))
-        deal_w4_scales(1, "w1bf1_0")
-        deal_w4_words(1, w4raw1, 0, PACK)
-        cast_w1(0, 1, raw01[:], 0, P, True)
-        quant_w1(0, 1, (0, KP))
+            nc.vector.tensor_copy(v_codes[a][:], tab[a][:].indirect(offs_sb[:]))
+        deal_w4(0, w4_raw0, "w4_plane0")
+        w4_raw1 = load_w4(1, "tab0")
+        w1_raw01 = load_w1(0, 1, "tab1")
+        for t0 in (0, 2):
+            cast_w1("scalar", 0, 0, w1_raw00[:], 0, P, t0, t0 + 2)
+        cast_w1("vector", 1, 0, w1_raw10[:, 0, :, :], 0, P // 2, 0, PACK)
+        quantise_w1(0, 0, 2)
+        for t0 in (0, 2):
+            cast_w1("scalar", 1, 0, w1_raw10[:, 1, :, :], P // 2, P, t0, t0 + 2)
+        w1_raw11 = load_w1(1, 1, "slot_b")
+        quantise_w1(1, 0, 2)
 
-        def load_w3(b, slot):
-            raw = held([P, PACK, N], F32, "w3raw%d" % b, slot)
-            nc.sync.dma_start(raw[:], w3[b * KP:(b + 1) * KP, :].rearrange("(p j) n -> p j n", j=PACK))
-            return raw
-
-        w3raw = [load_w3(0, "stage1"), load_w3(1, "tw1")]
-        w5_codes = held([P, 2, N], U32, "w5_codes", "stage2")
+        deal_w4(1, w4_raw1, "w1_bf10")
+        cast_w1("vector", 0, 1, w1_raw01[:], 0, P, 0, PACK)
+        quantise_w1(0, 1, PACK)
+        w3_raw = [load_rows("w3_raw%d" % b, slot, w3[b * PASS:(b + 1) * PASS, :])
+                  for b, slot in enumerate(("slot_a", "tab1"))]
+        w5_codes = held([P, 2, N], U32, "w5_codes", "slot_c")
         nc.sync.dma_start(w5_codes[:].bitcast(I32), w5_words.rearrange("b p n i -> p b (n i)").bitcast(I32))
 
-        def stage1(b, t, h1, h2):
+        def first_stage(b, t, h1, h2):
             cols = slice(t * P, (t + 1) * P)
-            sq = ring.tile([P, S], F32, name="sq")
-            for half in range(S // BANK):
-                js = slice(half * BANK, (half + 1) * BANK)
+            passes = [
+                (w4_codes[b][:, 0, cols].bitcast(E2M1), w4_plane[b][:, 0, cols], 0),
+                (w4_codes[b][:, 1, cols].bitcast(E2M1), w4_plane[b][:, 1, cols], 1),
+                (w1_codes[(0, b)][:, cols].bitcast(E4M3), w1_plane[(0, b)][:, cols], 0),
+                (w1_codes[(1, b)][:, cols].bitcast(E4M3), w1_plane[(1, b)][:, cols], 1),
+            ]
+            if b == 0 and t > 0:
+                passes = passes[::-1]
+            square = ring.tile([P, S], F32, name="square")
+            for j0 in range(0, S, BANK):
+                js = slice(j0, j0 + BANK)
                 acc = psum.tile([P, BANK], F32, name="acc")
-                passes = [
-                    (w4_codes[b][:, 0, cols].bitcast(E2M1), w4_plane[b][:, 0, cols], 0),
-                    (w4_codes[b][:, 1, cols].bitcast(E2M1), w4_plane[b][:, 1, cols], 1),
-                    (w1_codes[(0, b)][:, cols].bitcast(E4M3), w1_plane[(0, b)][:, cols], 0),
-                    (w1_codes[(1, b)][:, cols].bitcast(E4M3), w1_plane[(1, b)][:, cols], 1),
-                ]
-                for i, (codes, plane, a) in enumerate(passes):
+                for step, (codes, plane, a) in enumerate(passes):
                     nc.tensor.matmul_mx(acc[:], lhsT=codes, lhsT_scale=plane, rhs=v_codes[a][:, js].bitcast(E4M3),
-                                        rhs_scale=v_plane[:, a, js], start=(i == 0), stop=(i == len(passes) - 1))
-                nc.scalar.activation(sq[:, js], acc[:], ACT.Square, bias=zero[:])
-            if (b, t) == (1, 3):
-                lg = held([P, S], F32, "lg13", "late")
+                                        rhs_scale=v_plane[:, a, js], start=(step == 0),
+                                        stop=(step == len(passes) - 1))
+                nc.scalar.activation(square[:, js], acc[:], ACT.Square, bias=zero[:])
+            if (b, t) == (1, PACK - 1):
+                logs = held([P, S], F32, "last_logs", "slot_d")
             else:
-                lg = hring.tile([P, S], F32, name="lg")
-            h = hring.tile([P, S], F32, name="h")
-            step = BANK if (b, t) == (0, 0) else S
-            for j0 in range(0, S, step):
-                js = slice(j0, j0 + step)
-                nc.scalar.activation(lg[:, js], sq[:, js], ACT.Ln, bias=1.0)
-                if b == 0 and t < 2:
-                    nc.vector.tensor_scalar(h[:, js], lg[:, js], gain_sb[:, b, t:t + 1], None, ALU.mult)
-                else:
-                    nc.scalar.activation(h[:, js], lg[:, js], ACT.Copy, scale=gain_sb[:, b, t:t + 1])
+                logs = ahead.tile([P, S], F32, name="logs")
+            h = ahead.tile([P, S], F32, name="h")
+            nc.scalar.activation(logs[:], square[:], ACT.Ln, bias=1.0)
+            if PACK * b + t < GAINS_ON_VECTOR:
+                nc.vector.tensor_scalar(h[:], logs[:], gain_sb[:, b, t:t + 1], None, ALU.mult)
+            else:
+                nc.scalar.activation(h[:], logs[:], ACT.Copy, scale=gain_sb[:, b, t:t + 1])
             nc.vector.tensor_copy(h1[:, t, :], h[:].indirect(pos1_sb[:]))
             nc.vector.tensor_copy(h2[:, t, :], h[:].indirect(pos2_sb[:]))
 
-        HALF = PAIRS // 2
-
-        def join(b, half, h1, h2):
+        def join(half, h1, h2):
             ms = slice(half * HALF, (half + 1) * HALF)
-            bf = ring.tile([P, 2, HALF, PACK], BF16, name="pair_bf", align_bytes=64)
-            for i, op in enumerate((ALU.max, ALU.add)):
-                nc.vector.tensor_tensor(bf[:, i, :, :].rearrange("p (c i) t -> p c t i", i=4),
-                                        h1[:, :, ms].rearrange("p t (c i) -> p c t i", i=4),
-                                        h2[:, :, ms].rearrange("p t (c i) -> p c t i", i=4), op)
-            return bf
+            joined = ring.tile([P, 2, HALF, PACK], BF16, name="joined", align_bytes=64)
+            for kind, op in enumerate((ALU.max, ALU.add)):
+                nc.vector.tensor_tensor(joined[:, kind, :, :].rearrange("p (c e) t -> p c t e", e=LINE),
+                                        h1[:, :, ms].rearrange("p t (c e) -> p c t e", e=LINE),
+                                        h2[:, :, ms].rearrange("p t (c e) -> p c t e", e=LINE), op)
+            return joined
 
-        def quant_pair(b, half, bf):
-            codes = held([P, 2 * HALF], U32, "pair_codes%d_%d" % (b, half))
-            plane = held([P, 2 * HALF], U8, "pair_plane%d_%d" % (b, half))
-            nc.vector.quantize_mx(codes[:].bitcast(E4M3), plane[:], bf[:].rearrange("p i m t -> p (i m t)"))
+        def quantise_joined(b, half, joined):
+            codes = held([P, 2 * HALF], U32, "pair_codes%d%d" % (b, half))
+            plane = held([P, 2 * HALF], U8, "pair_plane%d%d" % (b, half))
+            nc.vector.quantize_mx(codes[:].bitcast(E4M3), plane[:], joined[:].rearrange("p kind m t -> p (kind m t)"))
             return codes, plane
 
-        pairs = {}
-        picked = []
-        for b in range(2):
-            h1 = ring.tile([P, PACK, PAIRS], F32, name="h1")
-            h2 = ring.tile([P, PACK, PAIRS], F32, name="h2")
-            picked.append((h1, h2))
-            for t in range(PACK):
-                stage1(b, t, h1, h2)
-                if b == 0 and t == 1:
-                    cast_w1(1, 1, raw11[:], 0, P, True)
-                    quant_w1(1, 1, (0, KP))
-            if b == 0:
-                made = [join(0, half, h1, h2) for half in range(2)]
-                for half in range(2):
-                    pairs[(0, half)] = quant_pair(0, half, made[half])
+        pair_operands = {}
 
-        w3_bf = held([P, 2, N, PACK], BF16, "w3_bf", "late")
+        h1 = ring.tile([P, PACK, PAIRS], F32, name="h1")
+        h2 = ring.tile([P, PACK, PAIRS], F32, name="h2")
+        for t in range(PACK):
+            first_stage(0, t, h1, h2)
+            if t == GAINS_ON_VECTOR - 1:
+                cast_w1("vector", 1, 1, w1_raw11[:], 0, P, 0, PACK)
+                quantise_w1(1, 1, PACK)
+        both_halves = [join(half, h1, h2) for half in range(2)]
+        for half in range(2):
+            pair_operands[(0, half)] = quantise_joined(0, half, both_halves[half])
+
+        h1 = ring.tile([P, PACK, PAIRS], F32, name="h1")
+        h2 = ring.tile([P, PACK, PAIRS], F32, name="h2")
+        for t in range(PACK):
+            first_stage(1, t, h1, h2)
+
+        w3_bf = held([P, 2, N, PACK], BF16, "w3_bf", "slot_d")
         w3_codes = held([P, 2 * N], U32, "w3_codes")
         w3_plane = held([P, 2 * N], U8, "w3_plane")
         for b in range(2):
-            nc.scalar.activation(
-                w3_bf[:, b, :, :].rearrange("p (c i) j -> p c j i", i=4),
-                w3raw[b][:].rearrange("p j (c i) -> p c j i", i=4), ACT.Copy, scale=-1.0)
-        first = join(1, 0, h1, h2)
-        flat = w3_bf[:].rearrange("p b n j -> p (b n j)")
-        for c0, width in ((0, 512), (512, 256)):
-            nc.vector.quantize_mx(w3_codes[:, c0:c0 + width].bitcast(E4M3), w3_plane[:, c0:c0 + width],
-                                  flat[:, PACK * c0:PACK * (c0 + width)])
-        pairs[(1, 0)] = quant_pair(1, 0, first)
-        pairs[(1, 1)] = quant_pair(1, 1, join(1, 1, h1, h2))
+            negate("scalar", w3_bf[:, b, :, :].rearrange("p (c e) i -> p c i e", e=LINE),
+                   w3_raw[b][:].rearrange("p i (c e) -> p c i e", e=LINE))
+        first_half = join(0, h1, h2)
+        w3_flat = w3_bf[:].rearrange("p b n i -> p (b n i)")
+        for c0, c1 in ((0, PASS), (PASS, 2 * N)):
+            nc.vector.quantize_mx(w3_codes[:, c0:c1].bitcast(E4M3), w3_plane[:, c0:c1],
+                                  w3_flat[:, PACK * c0:PACK * c1])
+        pair_operands[(1, 0)] = quantise_joined(1, 0, first_half)
+        pair_operands[(1, 1)] = quantise_joined(1, 1, join(1, h1, h2))
 
         for half in range(2):
             for n in range(N // P):
                 acc = psum.tile([P, HALF], F32, name="acc")
-                for b, i in ((0, 1), (0, 0), (1, 0), (1, 1)):
-                    codes, plane = pairs[(b, half)]
-                    cols3 = slice(b * N + n * P, b * N + (n + 1) * P)
-                    cols5 = slice(n * P, (n + 1) * P)
-                    weights = [(w3_codes[:, cols3], w3_plane[:, cols3]), (w5_codes[:, b, cols5], w5_plane[:, b, cols5])]
-                    w_codes, w_plane = weights[i]
-                    ms = slice(i * HALF, (i + 1) * HALF)
+                order = ((0, 1), (0, 0), (1, 0), (1, 1))
+                for step, (b, kind) in enumerate(order):
+                    codes, plane = pair_operands[(b, half)]
+                    if kind == 0:
+                        cols = slice(b * N + n * P, b * N + (n + 1) * P)
+                        w_codes, w_plane = w3_codes[:, cols], w3_plane[:, cols]
+                    else:
+                        cols = slice(n * P, (n + 1) * P)
+                        w_codes, w_plane = w5_codes[:, b, cols], w5_plane[:, b, cols]
+                    ms = slice(kind * HALF, (kind + 1) * HALF)
                     nc.tensor.matmul_mx(acc[:], lhsT=w_codes.bitcast(E4M3), lhsT_scale=w_plane,
                                         rhs=codes[:, ms].bitcast(E4M3), rhs_scale=plane[:, ms],
-                                        start=(b == 0 and i == 1), stop=(b == 1 and i == 1))
-                res = held([P, HALF], F32, "res%d_%d" % (half, n))
-                if half == 1 and n == 1:
-                    nc.vector.tensor_scalar(res[:], acc[:], -1.0, None, ALU.mult)
-                else:
-                    nc.scalar.activation(res[:], acc[:], ACT.Copy, scale=-1.0)
-                nc.sync.dma_start(out[n * P:(n + 1) * P, half * HALF:(half + 1) * HALF], res[:])
+                                        start=(step == 0), stop=(step == len(order) - 1))
+                result = held([P, HALF], F32, "result%d%d" % (half, n))
+                negate("vector" if (half, n) == (1, 1) else "scalar", result[:], acc[:])
+                nc.sync.dma_start(out[n * P:(n + 1) * P, half * HALF:(half + 1) * HALF], result[:])

from contextlib import ExitStack

import concourse.mybir as mybir

K, T, S, H, PAIRS, N = 1024, 2048, 1024, 1024, 512, 384
FLOPS = 2 * (2 * K * H * S + 2 * H * N * PAIRS)

F32 = mybir.dt.float32
BF16 = mybir.dt.bfloat16
I32 = mybir.dt.int32
U32 = mybir.dt.uint32
U16 = mybir.dt.uint16
U8 = mybir.dt.uint8
E4M3 = mybir.dt.float8_e4m3fn_x4
E2M1 = mybir.dt.float4_e2m1fn_x4
ACT = mybir.ActivationFunctionType
ALU = mybir.AluOpType

P = 128
PACK = 4
PASS = P * PACK
BANK = 512
QUADS, QUAD = 4, 32
LINE = 4
HALF = PAIRS // 2
GAINS_ON_VECTOR = 2


def tile_list_sneaker_doubt_pairs_kernel(tc, tab_words, tab_scales, offs, w1, w4_words, w4_scales, gain,
                                                  pos1, pos2, w3, w5_words, w5_scales, out):
    nc = tc.nc
    with ExitStack() as ctx:
        keep = ctx.enter_context(tc.tile_pool(name="keep", bufs=1))
        ring = ctx.enter_context(tc.tile_pool(name="ring", bufs=2))
        ahead = ctx.enter_context(tc.tile_pool(name="ahead", bufs=PACK))
        psum = ctx.enter_context(tc.psum_pool(name="psum", bufs=8))

        def held(shape, dtype, name, slot=None):
            return keep.tile(shape, dtype, name=name, tag=slot or name, align_bytes=64)

        offs_sb = keep.tile([P, S // 16], U16, name="offs_sb")
        pos1_sb = keep.tile([P, PAIRS // 16], U16, name="pos1_sb")
        pos2_sb = keep.tile([P, PAIRS // 16], U16, name="pos2_sb")

        tab_rows = held([P, T], U8, "tab_rows", "slot_a")
        w4_rows = held([P, 2, H], U8, "w4_rows")
        v_plane = held([P, 2, S], U8, "v_plane")
        w5_plane = held([P, 2, N], U8, "w5_plane")
        nc.vector.memset(tab_rows[:].bitcast(I32), 0)
        nc.vector.memset(w4_rows[:].rearrange("p a c -> p (a c)").bitcast(I32), 0)
        one = held([P, 1], F32, "one")
        zero = held([P, 1], F32, "zero")
        nc.vector.memset(one[:], 1.0)
        nc.vector.memset(v_plane[:].rearrange("p a c -> p (a c)").bitcast(I32), 0)
        nc.vector.memset(w5_plane[:].rearrange("p a c -> p (a c)").bitcast(I32), 0)

        nc.sync.dma_start(tab_rows[0:P:4, :].bitcast(I32), tab_scales.rearrange("a q t -> q a t").bitcast(I32))
        nc.sync.dma_start(offs_sb[:], offs)
        nc.sync.dma_start(pos1_sb[:], pos1)
        nc.sync.dma_start(pos2_sb[:], pos2)
        gain_sb = held([P, 2, PACK], F32, "gain_sb")

        def load_scale_rows(queue, plane, scales):
            for d in range(QUADS):
                queue.dma_start(plane[QUAD * d:QUAD * d + 4, :, :].bitcast(I32),
                                scales[:, 4 * d:4 * d + 4, :].rearrange("a q c -> q a c").bitcast(I32))

        load_scale_rows(nc.sync, w4_rows, w4_scales)
        nc.scalar.activation(zero[:], one[:], ACT.Ln)
        nc.gpsimd.dma_start(gain_sb[:], gain.rearrange("(b p t) -> p b t", b=2, t=PACK))
        load_scale_rows(nc.gpsimd, w5_plane, w5_scales)

        def load_rows(name, slot, rows):
            raw = held([P, PACK, rows.shape[1]], F32, name, slot)
            nc.sync.dma_start(raw[:], rows.rearrange("(p i) c -> p i c", i=PACK))
            return raw

        def load_w1(a, b, slot):
            return load_rows("w1_raw%d%d" % (a, b), slot, w1[a * PASS:(a + 1) * PASS, b * PASS:(b + 1) * PASS])

        def load_w4(b, slot):
            raw = held([P, 2, PASS], U16, "w4_raw%d" % b, slot)
            nc.sync.dma_start(raw[:].bitcast(I32),
                              w4_words[:, :, 2 * b * PASS:2 * (b + 1) * PASS].rearrange("a p c -> p a c").bitcast(I32))
            return raw

        w1_bf, w1_codes, w1_plane, w4_plane = {}, {}, {}, {}

        def negate(engine, dst, src):
            if engine == "vector":
                nc.vector.tensor_scalar(dst, src, -1.0, None, ALU.mult)
            else:
                nc.scalar.activation(dst, src, ACT.Copy, scale=-1.0)

        def cast_w1(engine, a, b, raw, m0, m1, t0, t1):
            if (a, b) not in w1_bf:
                w1_bf[(a, b)] = held([P, PACK, P, PACK], BF16, "w1_bf%d%d" % (a, b))
            negate(engine, w1_bf[(a, b)][:, t0:t1, m0:m1, :].rearrange("p t m i -> p m i t"),
                   raw.rearrange("p i (m t) -> p m i t", t=PACK)[:, :, :, t0:t1])

        def quantise_w1(a, b, slices_a_call):
            w1_codes[(a, b)] = held([P, PASS], U32, "w1_codes%d%d" % (a, b))
            w1_plane[(a, b)] = held([P, PASS], U8, "w1_plane%d%d" % (a, b))
            flat = w1_bf[(a, b)][:].rearrange("p t m i -> p (t m i)")
            for c0 in range(0, PASS, slices_a_call * P):
                c1 = c0 + slices_a_call * P
                nc.vector.quantize_mx(w1_codes[(a, b)][:, c0:c1].bitcast(E4M3), w1_plane[(a, b)][:, c0:c1],
                                      flat[:, PACK * c0:PACK * c1])

        def deal(dst, src):
            nc.vector.tensor_copy(dst.rearrange("p a (t m) -> p a t m", t=PACK),
                                  src.rearrange("p a (m t) -> p a t m", t=PACK))

        def deal_w4(b, raw, slot):
            w4_plane[b] = held([P, 2, PASS], U8, "w4_plane%d" % b, slot)
            deal(w4_plane[b][:], w4_rows[:, :, b * PASS:(b + 1) * PASS])
            deal(w4_codes[b][:], raw[:])

        tab = [held([P, T], U32, "tab%d" % a) for a in range(2)]
        w4_codes = [held([P, 2, PASS], U16, "w4_codes%d" % b) for b in range(2)]
        for a in range(2):
            nc.sync.dma_start(tab[a][:].bitcast(I32), tab_words[a].rearrange("p t i -> p (t i)").bitcast(I32))
        w4_raw0 = load_w4(0, "slot_c")
        w1_raw00 = load_w1(0, 0, "slot_b")

        v_rows = held([P, S], U8, "v_rows")
        nc.vector.tensor_copy(v_rows[:], tab_rows[:].indirect(offs_sb[:]))
        for d in range(QUADS):
            nc.sync.dma_start(v_plane[QUAD * d:QUAD * d + 4, :, :].bitcast(I32),
                              v_rows[QUAD * d:QUAD * (d + 1):4, :].bitcast(I32))
        w1_raw10 = held([P, 2, PACK, PASS // 2], F32, "w1_raw10", "slot_a")
        for u in range(2):
            nc.sync.dma_start(w1_raw10[:, u, :, :],
                              w1[PASS:2 * PASS, u * (PASS // 2):(u + 1) * (PASS // 2)].rearrange("(p i) c -> p i c", i=PACK))
        v_codes = [held([P, S], U32, "v_codes%d" % a) for a in range(2)]
        for a in range(2):
            nc.vector.tensor_copy(v_codes[a][:], tab[a][:].indirect(offs_sb[:]))
        deal_w4(0, w4_raw0, "w4_plane0")
        w4_raw1 = load_w4(1, "tab0")
        w1_raw01 = load_w1(0, 1, "tab1")
        for t0 in (0, 2):
            cast_w1("scalar", 0, 0, w1_raw00[:], 0, P, t0, t0 + 2)
        cast_w1("vector", 1, 0, w1_raw10[:, 0, :, :], 0, P // 2, 0, PACK)
        quantise_w1(0, 0, 2)
        for t0 in (0, 2):
            cast_w1("scalar", 1, 0, w1_raw10[:, 1, :, :], P // 2, P, t0, t0 + 2)
        w1_raw11 = load_w1(1, 1, "slot_b")
        quantise_w1(1, 0, 2)

        deal_w4(1, w4_raw1, "w1_bf10")
        cast_w1("vector", 0, 1, w1_raw01[:], 0, P, 0, PACK)
        quantise_w1(0, 1, PACK)
        w3_raw = [load_rows("w3_raw%d" % b, slot, w3[b * PASS:(b + 1) * PASS, :])
                  for b, slot in enumerate(("slot_a", "tab1"))]
        w5_codes = held([P, 2, N], U32, "w5_codes", "slot_c")
        nc.sync.dma_start(w5_codes[:].bitcast(I32), w5_words.rearrange("b p n i -> p b (n i)").bitcast(I32))

        def first_stage(b, t, h1, h2):
            cols = slice(t * P, (t + 1) * P)
            passes = [
                (w4_codes[b][:, 0, cols].bitcast(E2M1), w4_plane[b][:, 0, cols], 0),
                (w4_codes[b][:, 1, cols].bitcast(E2M1), w4_plane[b][:, 1, cols], 1),
                (w1_codes[(0, b)][:, cols].bitcast(E4M3), w1_plane[(0, b)][:, cols], 0),
                (w1_codes[(1, b)][:, cols].bitcast(E4M3), w1_plane[(1, b)][:, cols], 1),
            ]
            if b == 0 and t > 0:
                passes = passes[::-1]
            square = ring.tile([P, S], F32, name="square")
            for j0 in range(0, S, BANK):
                js = slice(j0, j0 + BANK)
                acc = psum.tile([P, BANK], F32, name="acc")
                for step, (codes, plane, a) in enumerate(passes):
                    nc.tensor.matmul_mx(acc[:], lhsT=codes, lhsT_scale=plane, rhs=v_codes[a][:, js].bitcast(E4M3),
                                        rhs_scale=v_plane[:, a, js], start=(step == 0),
                                        stop=(step == len(passes) - 1))
                nc.scalar.activation(square[:, js], acc[:], ACT.Square, bias=zero[:])
            if (b, t) == (1, PACK - 1):
                logs = held([P, S], F32, "last_logs", "slot_d")
            else:
                logs = ahead.tile([P, S], F32, name="logs")
            h = ahead.tile([P, S], F32, name="h")
            nc.scalar.activation(logs[:], square[:], ACT.Ln, bias=1.0)
            if PACK * b + t < GAINS_ON_VECTOR:
                nc.vector.tensor_scalar(h[:], logs[:], gain_sb[:, b, t:t + 1], None, ALU.mult)
            else:
                nc.scalar.activation(h[:], logs[:], ACT.Copy, scale=gain_sb[:, b, t:t + 1])
            nc.vector.tensor_copy(h1[:, t, :], h[:].indirect(pos1_sb[:]))
            nc.vector.tensor_copy(h2[:, t, :], h[:].indirect(pos2_sb[:]))

        def join(half, h1, h2):
            ms = slice(half * HALF, (half + 1) * HALF)
            joined = ring.tile([P, 2, HALF, PACK], BF16, name="joined", align_bytes=64)
            for kind, op in enumerate((ALU.max, ALU.add)):
                nc.vector.tensor_tensor(joined[:, kind, :, :].rearrange("p (c e) t -> p c t e", e=LINE),
                                        h1[:, :, ms].rearrange("p t (c e) -> p c t e", e=LINE),
                                        h2[:, :, ms].rearrange("p t (c e) -> p c t e", e=LINE), op)
            return joined

        def quantise_joined(b, half, joined):
            codes = held([P, 2 * HALF], U32, "pair_codes%d%d" % (b, half))
            plane = held([P, 2 * HALF], U8, "pair_plane%d%d" % (b, half))
            nc.vector.quantize_mx(codes[:].bitcast(E4M3), plane[:], joined[:].rearrange("p kind m t -> p (kind m t)"))
            return codes, plane

        pair_operands = {}

        h1 = ring.tile([P, PACK, PAIRS], F32, name="h1")
        h2 = ring.tile([P, PACK, PAIRS], F32, name="h2")
        for t in range(PACK):
            first_stage(0, t, h1, h2)
            if t == GAINS_ON_VECTOR - 1:
                cast_w1("vector", 1, 1, w1_raw11[:], 0, P, 0, PACK)
                quantise_w1(1, 1, PACK)
        both_halves = [join(half, h1, h2) for half in range(2)]
        for half in range(2):
            pair_operands[(0, half)] = quantise_joined(0, half, both_halves[half])

        h1 = ring.tile([P, PACK, PAIRS], F32, name="h1")
        h2 = ring.tile([P, PACK, PAIRS], F32, name="h2")
        for t in range(PACK):
            first_stage(1, t, h1, h2)

        w3_bf = held([P, 2, N, PACK], BF16, "w3_bf", "slot_d")
        w3_codes = held([P, 2 * N], U32, "w3_codes")
        w3_plane = held([P, 2 * N], U8, "w3_plane")
        for b in range(2):
            negate("scalar", w3_bf[:, b, :, :].rearrange("p (c e) i -> p c i e", e=LINE),
                   w3_raw[b][:].rearrange("p i (c e) -> p c i e", e=LINE))
        first_half = join(0, h1, h2)
        w3_flat = w3_bf[:].rearrange("p b n i -> p (b n i)")
        for c0, c1 in ((0, PASS), (PASS, 2 * N)):
            nc.vector.quantize_mx(w3_codes[:, c0:c1].bitcast(E4M3), w3_plane[:, c0:c1],
                                  w3_flat[:, PACK * c0:PACK * c1])
        pair_operands[(1, 0)] = quantise_joined(1, 0, first_half)
        pair_operands[(1, 1)] = quantise_joined(1, 1, join(1, h1, h2))

        for half in range(2):
            for n in range(N // P):
                acc = psum.tile([P, HALF], F32, name="acc")
                order = ((0, 1), (0, 0), (1, 0), (1, 1))
                for step, (b, kind) in enumerate(order):
                    codes, plane = pair_operands[(b, half)]
                    if kind == 0:
                        cols = slice(b * N + n * P, b * N + (n + 1) * P)
                        w_codes, w_plane = w3_codes[:, cols], w3_plane[:, cols]
                    else:
                        cols = slice(n * P, (n + 1) * P)
                        w_codes, w_plane = w5_codes[:, b, cols], w5_plane[:, b, cols]
                    ms = slice(kind * HALF, (kind + 1) * HALF)
                    nc.tensor.matmul_mx(acc[:], lhsT=w_codes.bitcast(E4M3), lhsT_scale=w_plane,
                                        rhs=codes[:, ms].bitcast(E4M3), rhs_scale=plane[:, ms],
                                        start=(step == 0), stop=(step == len(order) - 1))
                result = held([P, HALF], F32, "result%d%d" % (half, n))
                negate("vector" if (half, n) == (1, 1) else "scalar", result[:], acc[:])
                nc.sync.dma_start(out[n * P:(n + 1) * P, half * HALF:(half + 1) * HALF], result[:])
